import numpy as np
import ml_dtypes


def mxq(x, axis, fmt="e4m3"):
    dtype, down = {"e4m3": (ml_dtypes.float8_e4m3fn, 7), "e5m2": (ml_dtypes.float8_e5m2, 14)}[fmt]
    v = np.moveaxis(np.asarray(x, np.float32).astype(ml_dtypes.bfloat16).astype(np.float64), axis, -1)
    blocks = v.reshape(v.shape[:-1] + (-1, 32))
    amax = np.abs(blocks).max(-1, keepdims=True)
    byte = np.maximum(np.where(amax > 0, np.frexp(amax)[1] - 1 + 127, 0) - down, 1)
    scale = np.exp2(byte - 127.0)
    codes = (blocks / scale).astype(np.float32).astype(dtype).astype(np.float64)
    return np.moveaxis((codes * scale).reshape(v.shape), -1, axis)


WIDE = False


def mx_kscale(k):
    if not WIDE:
        return np.ones(k)
    levels = np.array([10, -10, 5, -5, 0])
    if k % 512:
        return np.exp2(np.random.permutation(np.resize(levels, k // 32))).repeat(32)
    a = np.empty((k // 512, 16))
    for p in range(k // 512):
        a[p, :8] = np.random.permutation(np.resize(levels, 8))
        for g in range(8):
            far = levels[np.abs(levels - a[p, g]) >= 10]
            a[p, g + 8] = far[np.random.randint(len(far))]
    return np.exp2(a.ravel()).repeat(32)


def f64(x):
    return np.asarray(x).astype(np.float64)


def striped(idx):
    return np.tile(idx.reshape(-1, 16).T, (8, 1)).astype(np.uint16)


def unstriped(offs):
    return offs[:16].T.reshape(-1).astype(np.int64)


def silu(v):
    return v / (1.0 + np.exp(-np.maximum(v, -700.0)))


K, T, E, C, H, N = 1024, 1280, 8, 128, 512, 256


def by_expert(wq, xq):
    return np.concatenate([wq[e].T @ xq[:, e * C:(e + 1) * C] for e in range(E)], axis=1)


def setup_inputs():
    n = np.random.standard_normal
    s = mx_kscale(K)[:, None]
    u = mx_kscale(H)
    return {
        "xT": (n((K, T)) * s).astype(np.float32),
        "w1": (n((E + 1, K, H)) / np.sqrt(K) / s[None] * u[None, None, :]).astype(np.float32),
        "w2": (n((E + 1, H, N)) / np.sqrt(H) / u[None, :, None]).astype(np.float32),
        "gate": np.tile(np.random.uniform(0.2, 1.0, E * C), (N, 1)).astype(np.float32),
        "offs": striped(np.random.permutation(T)[:E * C]),
    }


def reference(xT, w1, w2, gate, offs):
    idx = unstriped(offs)
    w1q, w2q = mxq(f64(w1), 1, "e4m3"), mxq(f64(w2), 1, "e4m3")
    xs = mxq(f64(xT), 0, "e4m3")
    hs = silu(w1q[E].T @ xs)
    ys = w2q[E].T @ mxq(hs, 0, "e4m3")
    xq = mxq(f64(xT)[:, idx], 0, "e4m3")
    h = silu(by_expert(w1q, xq))
    y = by_expert(w2q, mxq(h, 0, "e4m3"))
    out = ys
    out[:, idx] += f64(gate) * y
    return out

@@ -1,0 +1,377 @@
+from contextlib import ExitStack
+
+import concourse.mybir as mybir
+
+FLOPS = 3019898880
+
+K, T, E, C, H, N = 1024, 1280, 8, 128, 512, 256
+S = E * C
+SHARED = E
+
+F32 = mybir.dt.float32
+BF16 = mybir.dt.bfloat16
+U32 = mybir.dt.uint32
+U16 = mybir.dt.uint16
+U8 = mybir.dt.uint8
+FP8X4 = mybir.dt.float8_e4m3fn_x4
+SILU = mybir.ActivationFunctionType.Silu
+MULT = mybir.AluOpType.mult
+ADD = mybir.AluOpType.add
+
+P = 128
+PACK = 4
+PASS = P * PACK
+PASSES = K // PASS
+HALF = 512
+VECTOR_HALF = ((5, 1), (6, 1), (7, 1), (7, 0))
+PIECES = {3: (0, 256), 5: (256, 512), 7: (512, 768)}
+TAIL_PIECES = ((768, 1024),)
+CHUNKS = ((0, 256), (256, 512), (768, 512))
+
+
+def tile_moe_shr_mlp_silu_kernel(tc, xT, w1, w2, gate, offs, out):
+    nc = tc.nc
+    with ExitStack() as ctx:
+        lists = ctx.enter_context(tc.tile_pool(name="lists", bufs=1))
+        held = ctx.enter_context(tc.tile_pool(name="held", bufs=1))
+        ring = ctx.enter_context(tc.tile_pool(name="ring", bufs=2))
+        psum = ctx.enter_context(tc.psum_pool(name="psum", bufs=2))
+
+        offsets = lists.tile([P, S // 16], U16, name="offsets")
+        nc.sync.dma_start(offsets[:], offs)
+
+        zero = held.tile([P, 1], F32, name="zero")
+        zero_out = held.tile([P, 1], F32, name="zero_out")
+        nc.vector.memset(zero[:], 0.0)
+        nc.scalar.activation(zero_out[:], zero[:], SILU)
+
+        gates = held.tile([P, S], F32, name="gates", align_bytes=64)
+        routed = []
+        for b in range(2):
+            window = held.tile([P, T], F32, name=f"routed{b}", align_bytes=64)
+            nc.vector.memset(window[:], 0.0)
+            routed.append(window)
+
+        x_codes = held.tile([P, PASSES, T], U32, name="x_codes", align_bytes=64)
+        x_scales = held.tile([P, PASSES, T], U8, name="x_scales", align_bytes=64)
+        pairs = [held.tile([P, 2, T, 2], BF16, name=f"pairs{c}", align_bytes=64) for c in range(PASSES)]
+        g_codes = held.tile([P, PASSES, S], U32, name="g_codes", align_bytes=64)
+        g_scales = held.tile([P, PASSES, S], U8, name="g_scales", align_bytes=64)
+        hs_codes = held.tile([P, T], U32, name="hs_codes", align_bytes=64)
+        hs_scales = held.tile([P, T], U8, name="hs_scales", align_bytes=64)
+
+        raw = {}
+
+        def load_x(c, k):
+            start, width = CHUNKS[k]
+            if width == 512:
+                tile = ring.tile([P, PACK, 512], F32, name="raw_wide", tag="raw_wide", bufs=8, align_bytes=64)
+            else:
+                tile = ring.tile([P, PACK, 256], F32, name="raw_narrow", tag="raw_narrow", bufs=3, align_bytes=64)
+            rows = xT[c * PASS : (c + 1) * PASS, start : start + width]
+            nc.sync.dma_start(out=tile[:], in_=rows.rearrange("(p j) w -> p j w", j=PACK))
+            raw["x", c, k] = tile
+
+        def load_w1(e):
+            for c in range(PASSES):
+                tile = ring.tile([P, PACK, H], F32, name="raw_wide", tag="raw_wide", bufs=8, align_bytes=64)
+                nc.sync.dma_start(out=tile[:], in_=w1[e, c * PASS : (c + 1) * PASS, :].rearrange("(p j) w -> p j w", j=PACK))
+                raw["w1", e, c] = tile
+
+        def load_w2(e):
+            tile = ring.tile([P, PACK, N], F32, name="raw_narrow", tag="raw_narrow", bufs=3, align_bytes=64)
+            nc.sync.dma_start(out=tile[:], in_=w2[e].rearrange("(p j) w -> p j w", j=PACK))
+            raw["w2", e] = tile
+
+        def interleave(copy, dst, src):
+            copy(
+                out=dst.rearrange("p (c i) t -> p c t i", i=4),
+                in_=src.rearrange("p t (c i) -> p c t i", i=4),
+            )
+
+        grouped = {}
+
+        def group_x(c, k):
+            start, width = CHUNKS[k]
+            tile = ring.tile([P, 512, PACK], BF16, name="grouped_x", tag="grouped_x", bufs=3, align_bytes=64)
+            copy = nc.scalar.copy if width == 512 else nc.vector.tensor_copy
+            interleave(copy, tile[:, 0:width, :], raw["x", c, k][:])
+            grouped["x", c, k] = tile
+
+        def quantize_x(c, k):
+            start, width = CHUNKS[k]
+            cols = slice(start, start + width)
+            nc.vector.quantize_mx(
+                out=x_codes[:, c, cols].bitcast(FP8X4),
+                scales=x_scales[:, c, cols],
+                in_=grouped["x", c, k][:, 0:width, :].rearrange("p w t -> p (w t)"),
+            )
+
+        def pair_x(c, k):
+            start, width = CHUNKS[k]
+            nc.vector.tensor_copy(
+                out=pairs[c][:, :, start : start + width, :],
+                in_=grouped["x", c, k][:, 0:width, :].rearrange("p w (u e) -> p u w e", e=2),
+            )
+
+        looked_up = {}
+
+        def gather(c, half, u):
+            if u == 0:
+                looked_up[c, half] = ring.tile([P, 2, HALF, 2], BF16, name="gathered", tag="gathered", bufs=2, align_bytes=64)
+            window = pairs[c][:, u, :, :].rearrange("p t e -> p (t e)").bitcast(U32)
+            nc.vector.tensor_copy(
+                out=looked_up[c, half][:, u, :, :].rearrange("p t e -> p (t e)").bitcast(U32),
+                in_=window.indirect(offsets[:, half * (HALF // 16) : (half + 1) * (HALF // 16)]),
+            )
+
+        def group_g(c, half):
+            tile = ring.tile([P, HALF, PACK], BF16, name="grouped_g", tag="grouped_g", bufs=2, align_bytes=64)
+            nc.vector.tensor_copy(
+                out=tile[:].rearrange("p w (u e) -> p w u e", e=2),
+                in_=looked_up[c, half][:].rearrange("p u w e -> p w u e"),
+            )
+            grouped["g", c, half] = tile
+
+        def quantize_g(c, half):
+            cols = slice(half * HALF, (half + 1) * HALF)
+            nc.vector.quantize_mx(
+                out=g_codes[:, c, cols].bitcast(FP8X4),
+                scales=g_scales[:, c, cols],
+                in_=grouped["g", c, half][:].rearrange("p w t -> p (w t)"),
+            )
+
+        def group_w1(e, c):
+            tile = ring.tile([P, PACK * H], BF16, name="grouped_w1", tag="grouped_w1", bufs=4, align_bytes=64)
+            dst = tile[:].rearrange("p (t m j) -> p m j t", t=PACK, j=PACK)
+            src = raw["w1", e, c][:].rearrange("p j (m t) -> p m j t", t=PACK)
+            if (e, c) in VECTOR_HALF:
+                nc.vector.tensor_copy(out=dst[:, :, :, 0:2], in_=src[:, :, :, 0:2])
+                nc.scalar.copy(out=dst[:, :, :, 2:4], in_=src[:, :, :, 2:4])
+            else:
+                nc.scalar.copy(out=dst, in_=src)
+            grouped["w1", e, c] = tile
+
+        def group_w2(e, copy=nc.vector.tensor_copy):
+            tile = ring.tile([P, N, PACK], BF16, name="grouped_w2", tag="grouped_w2", bufs=3, align_bytes=64)
+            interleave(copy, tile[:], raw["w2", e][:])
+            grouped["w2", e] = tile
+
+        weights = {}
+
+        def quantize_w1(e):
+            if e == SHARED:
+                codes = held.tile([P, PASSES, H], U32, name="shared_codes", align_bytes=64)
+                scales = held.tile([P, PASSES, H], U8, name="shared_scales", align_bytes=64)
+            else:
+                codes = ring.tile([P, PASSES, H], U32, name="w1_codes", tag="w1_codes", bufs=2, align_bytes=64)
+                scales = ring.tile([P, PASSES, H], U8, name="w1_scales", tag="w1_scales", bufs=2, align_bytes=64)
+            for c in range(PASSES):
+                nc.vector.quantize_mx(out=codes[:, c, :].bitcast(FP8X4), scales=scales[:, c, :], in_=grouped["w1", e, c][:])
+            weights["w1", e] = (codes, scales)
+
+        def quantize_w2(e):
+            codes = ring.tile([P, N], U32, name="w2_codes", tag="w2_codes", bufs=4, align_bytes=64)
+            scales = ring.tile([P, N], U8, name="w2_scales", tag="w2_scales", bufs=4, align_bytes=64)
+            nc.vector.quantize_mx(
+                out=codes[:].bitcast(FP8X4), scales=scales[:], in_=grouped["w2", e][:].rearrange("p w t -> p (w t)")
+            )
+            weights["w2", e] = (codes, scales)
+
+        banks = {}
+        hidden = {}
+
+        def multiply1(key, e, codes, scales, start):
+            w_codes, w_scales = weights["w1", e]
+            cols = slice(start, start + C)
+            bank = psum.tile([P, PACK, C], F32, name="bank1", tag="bank1", bufs=4)
+            for t in range(PACK):
+                for c in range(PASSES):
+                    rows = slice(t * P, (t + 1) * P)
+                    nc.tensor.matmul_mx(
+                        out=bank[:, t, :],
+                        lhsT=w_codes[:, c, rows].bitcast(FP8X4),
+                        lhsT_scale=w_scales[:, c, rows],
+                        rhs=codes[:, c, cols].bitcast(FP8X4),
+                        rhs_scale=scales[:, c, cols],
+                        start=(c == 0),
+                        stop=(c == PASSES - 1),
+                    )
+            banks[key] = bank
+
+        def multiply1_routed(e):
+            multiply1(e, e, g_codes, g_scales, e * C)
+
+        def multiply1_shared(q):
+            for n in (2 * q, 2 * q + 1):
+                multiply1(("s", n), SHARED, x_codes, x_scales, n * C)
+
+        def silu_routed(e):
+            hidden[e] = ring.tile([P, C, PACK], BF16, name="hidden_routed", tag="hidden_routed", bufs=2, align_bytes=64)
+            nc.scalar.activation(hidden[e][:], banks[e][:].rearrange("p t n -> p n t"), SILU)
+
+        def silu_shared(q):
+            tile = ring.tile([P, 2 * C, PACK], BF16, name="hidden_shared", tag="hidden_shared", bufs=2, align_bytes=64)
+            for part in range(2):
+                nc.scalar.activation(
+                    tile[:, part * C : (part + 1) * C, :], banks["s", 2 * q + part][:].rearrange("p t n -> p n t"), SILU
+                )
+            hidden["s", q] = tile
+
+        def quantize_hs(q):
+            cols = slice(q * 2 * C, (q + 1) * 2 * C)
+            nc.vector.quantize_mx(
+                out=hs_codes[:, cols].bitcast(FP8X4),
+                scales=hs_scales[:, cols],
+                in_=hidden["s", q][:].rearrange("p w t -> p (w t)"),
+            )
+
+        hidden_codes = {}
+
+        def quantize_h(e):
+            codes = ring.tile([P, C], U32, name="h_codes", tag="h_codes", bufs=3, align_bytes=64)
+            scales = ring.tile([P, C], U8, name="h_scales", tag="h_scales", bufs=3, align_bytes=64)
+            nc.vector.quantize_mx(
+                out=codes[:].bitcast(FP8X4), scales=scales[:], in_=hidden[e][:].rearrange("p w t -> p (w t)")
+            )
+            hidden_codes[e] = (codes, scales)
+
+        y = held.tile([P, 2, S], F32, name="y", align_bytes=64)
+
+        def multiply2(e):
+            h_codes, h_scales = hidden_codes[e]
+            w_codes, w_scales = weights["w2", e]
+            bank = psum.tile([P, 2, C], F32, name="bank2", tag="bank2", bufs=2)
+            for b in range(2):
+                rows = slice(b * P, (b + 1) * P)
+                nc.tensor.matmul_mx(
+                    out=bank[:, b, :],
+                    lhsT=w_codes[:, rows].bitcast(FP8X4),
+                    lhsT_scale=w_scales[:, rows],
+                    rhs=h_codes[:].bitcast(FP8X4),
+                    rhs_scale=h_scales[:],
+                    start=True,
+                    stop=True,
+                )
+            banks["y", e] = bank
+
+        def copy_y(e):
+            nc.scalar.copy(out=y[:, :, e * C : (e + 1) * C], in_=banks["y", e][:])
+
+        def scatter(b, first, last):
+            nc.vector.tensor_tensor(
+                routed[b][:].indirect(offsets[:, first // 16 : last // 16]),
+                y[:, b, first:last],
+                gates[:, first:last],
+                MULT,
+            )
+
+        def finish(b, start, width):
+            w_codes, w_scales = weights["w2", SHARED]
+            rows = slice(b * P, (b + 1) * P)
+            cols = slice(start, start + width)
+            bank = psum.tile([P, 512], F32, name="bank3", tag="bank3", bufs=2)
+            nc.tensor.matmul_mx(
+                out=bank[:, 0:width],
+                lhsT=w_codes[:, rows].bitcast(FP8X4),
+                lhsT_scale=w_scales[:, rows],
+                rhs=hs_codes[:, cols].bitcast(FP8X4),
+                rhs_scale=hs_scales[:, cols],
+                start=True,
+                stop=True,
+            )
+            tile = ring.tile([P, 512], F32, name="total", tag="total", bufs=4, align_bytes=64)
+            nc.vector.tensor_tensor(tile[:, 0:width], bank[:, 0:width], routed[b][:, cols], ADD)
+            nc.sync.dma_start(out=out[rows, cols], in_=tile[:, 0:width])
+
+        for c in range(PASSES):
+            for k in range(3):
+                load_x(c, k)
+        load_w1(SHARED)
+        load_w1(0)
+        load_w2(0)
+
+        for k in range(3):
+            group_x(0, k)
+        for k in range(2):
+            quantize_x(0, k)
+            pair_x(0, k)
+        load_w1(1)
+        load_w2(1)
+        nc.sync.dma_start(out=gates[:], in_=gate[0:P, :])
+        group_x(1, 0)
+        quantize_x(0, 2)
+        pair_x(0, 2)
+        gather(0, 0, 0)
+        quantize_x(1, 0)
+        pair_x(1, 0)
+        gather(0, 0, 1)
+        group_x(1, 1)
+        group_x(1, 2)
+        group_w1(SHARED, 0)
+        quantize_x(1, 1)
+        pair_x(1, 1)
+        group_g(0, 0)
+        gather(0, 1, 0)
+        quantize_g(0, 0)
+        quantize_x(1, 2)
+        pair_x(1, 2)
+        load_w1(2)
+        load_w2(2)
+        group_w1(SHARED, 1)
+        load_w1(3)
+        gather(1, 0, 0)
+        gather(1, 0, 1)
+
+        extra = {
+            0: lambda: (group_g(1, 0), gather(0, 1, 1), quantize_g(1, 0)),
+            1: lambda: (gather(1, 1, 0), group_g(0, 1)),
+            2: lambda: (quantize_g(0, 1), gather(1, 1, 1)),
+            3: lambda: (group_g(1, 1),),
+            4: lambda: (quantize_g(1, 1),),
+        }
+        for i in range(E + 1):
+            prev = SHARED if i == 0 else i - 1
+            quantize_w1(prev)
+            if i > 0:
+                quantize_w2(prev)
+            if i >= 2:
+                quantize_h(i - 2)
+            if 2 <= i <= 6:
+                quantize_hs(i - 2)
+            if i < E:
+                group_w1(i, 0)
+            if i > 0:
+                multiply1_routed(i - 1)
+            if 2 <= i:
+                multiply2(i - 2)
+                copy_y(i - 2)
+            if i < E:
+                group_w1(i, 1)
+            if i > 0:
+                silu_routed(i - 1)
+            if 1 <= i <= 5:
+                multiply1_shared(i - 1)
+                silu_shared(i - 1)
+            if i in extra:
+                extra[i]()
+            if i in PIECES:
+                for b in range(2):
+                    scatter(b, *PIECES[i])
+            if i < E:
+                group_w2(i)
+            if i + 3 <= E:
+                load_w2(i + 3)
+            if i + 4 < E:
+                load_w1(i + 4)
+
+        group_w2(SHARED, nc.scalar.copy)
+        quantize_h(7)
+        quantize_w2(SHARED)
+        multiply2(7)
+        copy_y(7)
+        for b in range(2):
+            for piece in TAIL_PIECES:
+                scatter(b, *piece)
+            for start, width in ((0, 512), (512, 512), (1024, 256)):
+                finish(b, start, width)

@@ -23,9 +23,17 @@ PACK = 4
 PASS = P * PACK
 PASSES = K // PASS
 HALF = 512
-VECTOR_HALF = ((5, 1), (6, 1), (7, 1), (7, 0))
-PIECES = {3: (0, 256), 5: (256, 512), 7: (512, 768)}
-TAIL_PIECES = ((768, 1024),)
+VECTOR_HALF = ((4, 1), (5, 1), (6, 1))
+VECTOR_X = ((0, 0), (1, 0))
+SCALAR_W2 = ()
+PIECES = {4: (0, 256), 6: (256, 512)}
+TAIL_PIECES = ((512, 864), (864, 1024))
+SH0 = 1
+LATE_GATHER = 1
+FINISH = (
+    ((0, 512, "bank3"), (512, 512, "bank3"), (1024, 256, "bank_shared")),
+    ((0, 512, "bank_shared"), (512, 512, "bank_routed"), (1024, 256, "bank_routed")),
+)
 CHUNKS = ((0, 256), (256, 512), (768, 512))
 
 
@@ -62,6 +70,9 @@ def tile_moe_shr_mlp_silu_kernel(tc, xT, w1, w2, gate, offs, out):
 
         raw = {}
 
+        def load_gates():
+            nc.sync.dma_start(out=gates[:], in_=gate[0:P, :])
+
         def load_x(c, k):
             start, width = CHUNKS[k]
             if width == 512:
@@ -94,7 +105,7 @@ def tile_moe_shr_mlp_silu_kernel(tc, xT, w1, w2, gate, offs, out):
         def group_x(c, k):
             start, width = CHUNKS[k]
             tile = ring.tile([P, 512, PACK], BF16, name="grouped_x", tag="grouped_x", bufs=3, align_bytes=64)
-            copy = nc.scalar.copy if width == 512 else nc.vector.tensor_copy
+            copy = nc.vector.tensor_copy if (c, k) in VECTOR_X else nc.scalar.copy
             interleave(copy, tile[:, 0:width, :], raw["x", c, k][:])
             grouped["x", c, k] = tile
 
@@ -117,8 +128,12 @@ def tile_moe_shr_mlp_silu_kernel(tc, xT, w1, w2, gate, offs, out):
         looked_up = {}
 
         def gather(c, half, u):
-            if u == 0:
-                looked_up[c, half] = ring.tile([P, 2, HALF, 2], BF16, name="gathered", tag="gathered", bufs=2, align_bytes=64)
+            if u == 0 and half == 0:
+                tile = ring.tile([P, 2, HALF, 2], BF16, name="gathered", tag="gathered", bufs=2, align_bytes=64)
+                looked_up[c, half] = tile[:]
+            elif u == 0:
+                words = raw["w1", LATE_GATHER + c, 0][:].rearrange("p j w -> p (j w)")[:, 2 * HALF : 4 * HALF]
+                looked_up[c, half] = words.bitcast(BF16).rearrange("p (u n e) -> p u n e", u=2, e=2)
             window = pairs[c][:, u, :, :].rearrange("p t e -> p (t e)").bitcast(U32)
             nc.vector.tensor_copy(
                 out=looked_up[c, half][:, u, :, :].rearrange("p t e -> p (t e)").bitcast(U32),
@@ -129,7 +144,7 @@ def tile_moe_shr_mlp_silu_kernel(tc, xT, w1, w2, gate, offs, out):
             tile = ring.tile([P, HALF, PACK], BF16, name="grouped_g", tag="grouped_g", bufs=2, align_bytes=64)
             nc.vector.tensor_copy(
                 out=tile[:].rearrange("p w (u e) -> p w u e", e=2),
-                in_=looked_up[c, half][:].rearrange("p u w e -> p w u e"),
+                in_=looked_up[c, half].rearrange("p u w e -> p w u e"),
             )
             grouped["g", c, half] = tile
 
@@ -142,7 +157,7 @@ def tile_moe_shr_mlp_silu_kernel(tc, xT, w1, w2, gate, offs, out):
             )
 
         def group_w1(e, c):
-            tile = ring.tile([P, PACK * H], BF16, name="grouped_w1", tag="grouped_w1", bufs=4, align_bytes=64)
+            tile = ring.tile([P, PACK * H], BF16, name="grouped_w1", tag="grouped_w1", bufs=6, align_bytes=64)
             dst = tile[:].rearrange("p (t m j) -> p m j t", t=PACK, j=PACK)
             src = raw["w1", e, c][:].rearrange("p j (m t) -> p m j t", t=PACK)
             if (e, c) in VECTOR_HALF:
@@ -152,7 +167,8 @@ def tile_moe_shr_mlp_silu_kernel(tc, xT, w1, w2, gate, offs, out):
                 nc.scalar.copy(out=dst, in_=src)
             grouped["w1", e, c] = tile
 
-        def group_w2(e, copy=nc.vector.tensor_copy):
+        def group_w2(e):
+            copy = nc.scalar.copy if e in SCALAR_W2 else nc.vector.tensor_copy
             tile = ring.tile([P, N, PACK], BF16, name="grouped_w2", tag="grouped_w2", bufs=3, align_bytes=64)
             interleave(copy, tile[:], raw["w2", e][:])
             grouped["w2", e] = tile
@@ -181,10 +197,10 @@ def tile_moe_shr_mlp_silu_kernel(tc, xT, w1, w2, gate, offs, out):
         banks = {}
         hidden = {}
 
-        def multiply1(key, e, codes, scales, start):
+        def multiply1(key, e, codes, scales, start, tag):
             w_codes, w_scales = weights["w1", e]
             cols = slice(start, start + C)
-            bank = psum.tile([P, PACK, C], F32, name="bank1", tag="bank1", bufs=4)
+            bank = psum.tile([P, PACK, C], F32, name="bank1", tag=tag, bufs=2)
             for t in range(PACK):
                 for c in range(PASSES):
                     rows = slice(t * P, (t + 1) * P)
@@ -200,18 +216,25 @@ def tile_moe_shr_mlp_silu_kernel(tc, xT, w1, w2, gate, offs, out):
             banks[key] = bank
 
         def multiply1_routed(e):
-            multiply1(e, e, g_codes, g_scales, e * C)
+            multiply1(e, e, g_codes, g_scales, e * C, "bank_routed")
 
         def multiply1_shared(q):
             for n in (2 * q, 2 * q + 1):
-                multiply1(("s", n), SHARED, x_codes, x_scales, n * C)
+                multiply1(("s", n), SHARED, x_codes, x_scales, n * C, "bank_shared")
+
+        def freed(e, c, first, last):
+            return raw["w1", e, c][:].rearrange("p j w -> p (j w)")[:, first:last].bitcast(BF16).rearrange("p (n t) -> p n t", t=PACK)
 
         def silu_routed(e):
-            hidden[e] = ring.tile([P, C, PACK], BF16, name="hidden_routed", tag="hidden_routed", bufs=2, align_bytes=64)
-            nc.scalar.activation(hidden[e][:], banks[e][:].rearrange("p t n -> p n t"), SILU)
+            if e + 2 < E:
+                hidden[e] = freed(e + 2, 1, 0, 256)
+            else:
+                tile = ring.tile([P, C, PACK], BF16, name="hidden_routed", tag="hidden_routed", bufs=2, align_bytes=64)
+                hidden[e] = tile[:]
+            nc.scalar.activation(hidden[e], banks[e][:].rearrange("p t n -> p n t"), SILU)
 
         def silu_shared(q):
-            tile = ring.tile([P, 2 * C, PACK], BF16, name="hidden_shared", tag="hidden_shared", bufs=2, align_bytes=64)
+            tile = freed(q + SH0 + 1, 1, 256, 768)
             for part in range(2):
                 nc.scalar.activation(
                     tile[:, part * C : (part + 1) * C, :], banks["s", 2 * q + part][:].rearrange("p t n -> p n t"), SILU
@@ -223,7 +246,7 @@ def tile_moe_shr_mlp_silu_kernel(tc, xT, w1, w2, gate, offs, out):
             nc.vector.quantize_mx(
                 out=hs_codes[:, cols].bitcast(FP8X4),
                 scales=hs_scales[:, cols],
-                in_=hidden["s", q][:].rearrange("p w t -> p (w t)"),
+                in_=hidden["s", q].rearrange("p w t -> p (w t)"),
             )
 
         hidden_codes = {}
@@ -232,11 +255,12 @@ def tile_moe_shr_mlp_silu_kernel(tc, xT, w1, w2, gate, offs, out):
             codes = ring.tile([P, C], U32, name="h_codes", tag="h_codes", bufs=3, align_bytes=64)
             scales = ring.tile([P, C], U8, name="h_scales", tag="h_scales", bufs=3, align_bytes=64)
             nc.vector.quantize_mx(
-                out=codes[:].bitcast(FP8X4), scales=scales[:], in_=hidden[e][:].rearrange("p w t -> p (w t)")
+                out=codes[:].bitcast(FP8X4), scales=scales[:], in_=hidden[e].rearrange("p w t -> p (w t)")
             )
             hidden_codes[e] = (codes, scales)
 
-        y = held.tile([P, 2, S], F32, name="y", align_bytes=64)
+        y_last = held.tile([P, 2, 4 * C], F32, name="y_last", align_bytes=64)
+        y_place = {}
 
         def multiply2(e):
             h_codes, h_scales = hidden_codes[e]
@@ -256,21 +280,28 @@ def tile_moe_shr_mlp_silu_kernel(tc, xT, w1, w2, gate, offs, out):
             banks["y", e] = bank
 
         def copy_y(e):
-            nc.scalar.copy(out=y[:, :, e * C : (e + 1) * C], in_=banks["y", e][:])
+            if e < 4:
+                flat = raw["w1", 4 + 2 * (e // 2), 0][:].rearrange("p j w -> p (j w)")[:, 0:512].rearrange("p (b n) -> p b n", b=2)
+                y_place[e] = (flat, e // 2 * 2 * C)
+            else:
+                y_place[e] = (y_last[:], 4 * C)
+            place, base = y_place[e]
+            nc.scalar.copy(out=place[:, :, e * C - base : (e + 1) * C - base], in_=banks["y", e][:])
 
         def scatter(b, first, last):
+            place, base = y_place[first // C]
             nc.vector.tensor_tensor(
                 routed[b][:].indirect(offsets[:, first // 16 : last // 16]),
-                y[:, b, first:last],
+                place[:, b, first - base : last - base],
                 gates[:, first:last],
                 MULT,
             )
 
-        def finish(b, start, width):
+        def finish(b, start, width, tag):
             w_codes, w_scales = weights["w2", SHARED]
             rows = slice(b * P, (b + 1) * P)
             cols = slice(start, start + width)
-            bank = psum.tile([P, 512], F32, name="bank3", tag="bank3", bufs=2)
+            bank = psum.tile([P, 512], F32, name="bank3", tag=tag, bufs=2)
             nc.tensor.matmul_mx(
                 out=bank[:, 0:width],
                 lhsT=w_codes[:, rows].bitcast(FP8X4),
@@ -289,89 +320,94 @@ def tile_moe_shr_mlp_silu_kernel(tc, xT, w1, w2, gate, offs, out):
                 load_x(c, k)
         load_w1(SHARED)
         load_w1(0)
-        load_w2(0)
 
-        for k in range(3):
-            group_x(0, k)
-        for k in range(2):
-            quantize_x(0, k)
-            pair_x(0, k)
+        group_x(0, 0)
+        group_x(0, 1)
+        quantize_x(0, 0)
+        pair_x(0, 0)
+        group_x(0, 2)
         load_w1(1)
-        load_w2(1)
-        nc.sync.dma_start(out=gates[:], in_=gate[0:P, :])
+        load_w2(0)
+        quantize_x(0, 1)
+        pair_x(0, 1)
         group_x(1, 0)
+        group_x(1, 1)
         quantize_x(0, 2)
         pair_x(0, 2)
-        gather(0, 0, 0)
         quantize_x(1, 0)
         pair_x(1, 0)
-        gather(0, 0, 1)
-        group_x(1, 1)
+        gather(0, 0, 0)
         group_x(1, 2)
-        group_w1(SHARED, 0)
+        gather(0, 0, 1)
         quantize_x(1, 1)
         pair_x(1, 1)
+        group_w1(SHARED, 0)
         group_g(0, 0)
-        gather(0, 1, 0)
-        quantize_g(0, 0)
         quantize_x(1, 2)
         pair_x(1, 2)
         load_w1(2)
-        load_w2(2)
+        load_w2(1)
         group_w1(SHARED, 1)
         load_w1(3)
+        load_gates()
+        quantize_g(0, 0)
         gather(1, 0, 0)
         gather(1, 0, 1)
 
         extra = {
-            0: lambda: (group_g(1, 0), gather(0, 1, 1), quantize_g(1, 0)),
-            1: lambda: (gather(1, 1, 0), group_g(0, 1)),
-            2: lambda: (quantize_g(0, 1), gather(1, 1, 1)),
-            3: lambda: (group_g(1, 1),),
+            0: lambda: (group_g(1, 0), quantize_g(1, 0)),
+            1: lambda: (gather(0, 1, 0), gather(0, 1, 1)),
+            2: lambda: (group_g(0, 1), gather(1, 1, 0), gather(1, 1, 1)),
+            3: lambda: (quantize_g(0, 1), group_g(1, 1)),
             4: lambda: (quantize_g(1, 1),),
         }
-        for i in range(E + 1):
+        for i in range(E + 2):
             prev = SHARED if i == 0 else i - 1
-            quantize_w1(prev)
-            if i > 0:
-                quantize_w2(prev)
-            if i >= 2:
-                quantize_h(i - 2)
-            if 2 <= i <= 6:
-                quantize_hs(i - 2)
+            if i <= E:
+                quantize_w1(prev)
+                if i > 0:
+                    quantize_w2(prev)
             if i < E:
                 group_w1(i, 0)
-            if i > 0:
-                multiply1_routed(i - 1)
-            if 2 <= i:
-                multiply2(i - 2)
-                copy_y(i - 2)
-            if i < E:
                 group_w1(i, 1)
-            if i > 0:
-                silu_routed(i - 1)
-            if 1 <= i <= 5:
-                multiply1_shared(i - 1)
-                silu_shared(i - 1)
+            if i in (4, 6, 8):
+                copy_y(i - 4)
+                copy_y(i - 3)
+            if i >= 2:
+                silu_routed(i - 2)
+            if 0 <= i - SH0 - 1 < 5:
+                silu_shared(i - SH0 - 1)
+            if i in PIECES:
+                scatter(0, *PIECES[i])
+            if i >= 2:
+                quantize_h(i - 2)
+            if 0 <= i - SH0 - 1 < 5:
+                quantize_hs(i - SH0 - 1)
             if i in extra:
                 extra[i]()
+            if 1 <= i <= E:
+                multiply1_routed(i - 1)
+            if i >= 2:
+                multiply2(i - 2)
+            if 0 <= i - SH0 < 5:
+                multiply1_shared(i - SH0)
             if i in PIECES:
-                for b in range(2):
-                    scatter(b, *PIECES[i])
+                scatter(1, *PIECES[i])
             if i < E:
                 group_w2(i)
-            if i + 3 <= E:
-                load_w2(i + 3)
-            if i + 4 < E:
-                load_w1(i + 4)
+            if i == E - 1:
+                group_w2(SHARED)
+            if i == E:
+                quantize_w2(SHARED)
+            if i + 2 <= E:
+                load_w2(i + 2)
+            if 1 <= i and i + 3 < E:
+                load_w1(i + 3)
 
-        group_w2(SHARED, nc.scalar.copy)
-        quantize_h(7)
-        quantize_w2(SHARED)
-        multiply2(7)
+        copy_y(6)
         copy_y(7)
         for b in range(2):
             for piece in TAIL_PIECES:
                 scatter(b, *piece)
-            for start, width in ((0, 512), (512, 512), (1024, 256)):
-                finish(b, start, width)
+            for start, width, tag in FINISH[b]:
+                finish(b, start, width, tag)

@@ -23,18 +23,17 @@ PACK = 4
 PASS = P * PACK
 PASSES = K // PASS
 HALF = 512
-VECTOR_HALF = ((4, 1), (5, 1), (6, 1))
-VECTOR_X = ((0, 0), (1, 0))
-SCALAR_W2 = ()
-PIECES = {4: (0, 256), 6: (256, 512)}
-TAIL_PIECES = ((512, 864), (864, 1024))
-SH0 = 1
-LATE_GATHER = 1
+VECTOR_HALF = ((2, 0), (2, 1), (3, 0), (3, 1), (4, 0), (5, 0), (6, 0), (7, 0))
+SCALAR_W2 = (7, 8)
+PIECES = {3: (0, 256), 5: (256, 512), 7: (512, 768)}
+TAIL_PIECES = ((768, 1024),)
+SHARED_STEP = (1, 2, 3, 4, 5)
 FINISH = (
     ((0, 512, "bank3"), (512, 512, "bank3"), (1024, 256, "bank_shared")),
     ((0, 512, "bank_shared"), (512, 512, "bank_routed"), (1024, 256, "bank_routed")),
 )
-CHUNKS = ((0, 256), (256, 512), (768, 512))
+CHUNKS = ((0, 512), (512, 512), (1024, 256))
+VECTOR_X = ((0, 0, 0), (0, 0, 1))
 
 
 def tile_moe_shr_mlp_silu_kernel(tc, xT, w1, w2, gate, offs, out):
@@ -73,21 +72,16 @@ def tile_moe_shr_mlp_silu_kernel(tc, xT, w1, w2, gate, offs, out):
         def load_gates():
             nc.sync.dma_start(out=gates[:], in_=gate[0:P, :])
 
-        def load_x(c, k):
-            start, width = CHUNKS[k]
-            if width == 512:
-                tile = ring.tile([P, PACK, 512], F32, name="raw_wide", tag="raw_wide", bufs=8, align_bytes=64)
-            else:
-                tile = ring.tile([P, PACK, 256], F32, name="raw_narrow", tag="raw_narrow", bufs=3, align_bytes=64)
-            rows = xT[c * PASS : (c + 1) * PASS, start : start + width]
-            nc.sync.dma_start(out=tile[:], in_=rows.rearrange("(p j) w -> p j w", j=PACK))
-            raw["x", c, k] = tile
+        def load_x(c, u, h):
+            tile = ring.tile([P, 2, T // 2], F32, name="raw_x", tag="raw_x", bufs=4, align_bytes=64)
+            rows = xT[c * PASS : (c + 1) * PASS, h * (T // 2) : (h + 1) * (T // 2)].rearrange("(p u e) w -> u p e w", u=2, e=2)
+            nc.sync.dma_start(out=tile[:], in_=rows[u])
+            raw["x", c, u, h] = tile
 
-        def load_w1(e):
-            for c in range(PASSES):
-                tile = ring.tile([P, PACK, H], F32, name="raw_wide", tag="raw_wide", bufs=8, align_bytes=64)
-                nc.sync.dma_start(out=tile[:], in_=w1[e, c * PASS : (c + 1) * PASS, :].rearrange("(p j) w -> p j w", j=PACK))
-                raw["w1", e, c] = tile
+        def load_w1(e, c):
+            tile = ring.tile([P, PACK, H], F32, name="raw_wide", tag="raw_wide", bufs=7, align_bytes=64)
+            nc.sync.dma_start(out=tile[:], in_=w1[e, c * PASS : (c + 1) * PASS, :].rearrange("(p j) w -> p j w", j=PACK))
+            raw["w1", e, c] = tile
 
         def load_w2(e):
             tile = ring.tile([P, PACK, N], F32, name="raw_narrow", tag="raw_narrow", bufs=3, align_bytes=64)
@@ -102,11 +96,20 @@ def tile_moe_shr_mlp_silu_kernel(tc, xT, w1, w2, gate, offs, out):
 
         grouped = {}
 
+        def pair_x(c, u, h):
+            copy = nc.vector.tensor_copy if (c, u, h) in VECTOR_X else nc.scalar.copy
+            copy(
+                out=pairs[c][:, u, h * (T // 2) : (h + 1) * (T // 2), :].rearrange("p (c i) e -> p c e i", i=4),
+                in_=raw["x", c, u, h][:].rearrange("p e (c i) -> p c e i", i=4),
+            )
+
         def group_x(c, k):
             start, width = CHUNKS[k]
-            tile = ring.tile([P, 512, PACK], BF16, name="grouped_x", tag="grouped_x", bufs=3, align_bytes=64)
-            copy = nc.vector.tensor_copy if (c, k) in VECTOR_X else nc.scalar.copy
-            interleave(copy, tile[:, 0:width, :], raw["x", c, k][:])
+            tile = ring.tile([P, 512, PACK], BF16, name="grouped_x", tag="grouped_x", bufs=2, align_bytes=64)
+            nc.vector.tensor_copy(
+                out=tile[:, 0:width, :].rearrange("p w (u e) -> p w u e", e=2),
+                in_=pairs[c][:, :, start : start + width, :].rearrange("p u w e -> p w u e"),
+            )
             grouped["x", c, k] = tile
 
         def quantize_x(c, k):
@@ -118,22 +121,11 @@ def tile_moe_shr_mlp_silu_kernel(tc, xT, w1, w2, gate, offs, out):
                 in_=grouped["x", c, k][:, 0:width, :].rearrange("p w t -> p (w t)"),
             )
 
-        def pair_x(c, k):
-            start, width = CHUNKS[k]
-            nc.vector.tensor_copy(
-                out=pairs[c][:, :, start : start + width, :],
-                in_=grouped["x", c, k][:, 0:width, :].rearrange("p w (u e) -> p u w e", e=2),
-            )
-
         looked_up = {}
 
         def gather(c, half, u):
-            if u == 0 and half == 0:
-                tile = ring.tile([P, 2, HALF, 2], BF16, name="gathered", tag="gathered", bufs=2, align_bytes=64)
-                looked_up[c, half] = tile[:]
-            elif u == 0:
-                words = raw["w1", LATE_GATHER + c, 0][:].rearrange("p j w -> p (j w)")[:, 2 * HALF : 4 * HALF]
-                looked_up[c, half] = words.bitcast(BF16).rearrange("p (u n e) -> p u n e", u=2, e=2)
+            if u == 0:
+                looked_up[c, half] = ring.tile([P, 2, HALF, 2], BF16, name="gathered", tag="gathered", bufs=2, align_bytes=64)
             window = pairs[c][:, u, :, :].rearrange("p t e -> p (t e)").bitcast(U32)
             nc.vector.tensor_copy(
                 out=looked_up[c, half][:, u, :, :].rearrange("p t e -> p (t e)").bitcast(U32),
@@ -144,7 +136,7 @@ def tile_moe_shr_mlp_silu_kernel(tc, xT, w1, w2, gate, offs, out):
             tile = ring.tile([P, HALF, PACK], BF16, name="grouped_g", tag="grouped_g", bufs=2, align_bytes=64)
             nc.vector.tensor_copy(
                 out=tile[:].rearrange("p w (u e) -> p w u e", e=2),
-                in_=looked_up[c, half].rearrange("p u w e -> p w u e"),
+                in_=looked_up[c, half][:].rearrange("p u w e -> p w u e"),
             )
             grouped["g", c, half] = tile
 
@@ -226,15 +218,19 @@ def tile_moe_shr_mlp_silu_kernel(tc, xT, w1, w2, gate, offs, out):
             return raw["w1", e, c][:].rearrange("p j w -> p (j w)")[:, first:last].bitcast(BF16).rearrange("p (n t) -> p n t", t=PACK)
 
         def silu_routed(e):
-            if e + 2 < E:
-                hidden[e] = freed(e + 2, 1, 0, 256)
+            if e + 1 < E:
+                hidden[e] = freed(e + 1, 1, 0, 256)
             else:
                 tile = ring.tile([P, C, PACK], BF16, name="hidden_routed", tag="hidden_routed", bufs=2, align_bytes=64)
                 hidden[e] = tile[:]
             nc.scalar.activation(hidden[e], banks[e][:].rearrange("p t n -> p n t"), SILU)
 
         def silu_shared(q):
-            tile = freed(q + SH0 + 1, 1, 256, 768)
+            if SHARED_STEP[q] < E:
+                tile = freed(SHARED_STEP[q], 1, 256, 768)
+            else:
+                own = ring.tile([P, 2 * C, PACK], BF16, name="hidden_shared", tag="hidden_shared", bufs=2, align_bytes=64)
+                tile = own[:]
             for part in range(2):
                 nc.scalar.activation(
                     tile[:, part * C : (part + 1) * C, :], banks["s", 2 * q + part][:].rearrange("p t n -> p n t"), SILU
@@ -259,7 +255,7 @@ def tile_moe_shr_mlp_silu_kernel(tc, xT, w1, w2, gate, offs, out):
             )
             hidden_codes[e] = (codes, scales)
 
-        y_last = held.tile([P, 2, 4 * C], F32, name="y_last", align_bytes=64)
+        y_last = held.tile([P, 2, 2 * C], F32, name="y_last", align_bytes=64)
         y_place = {}
 
         def multiply2(e):
@@ -280,11 +276,11 @@ def tile_moe_shr_mlp_silu_kernel(tc, xT, w1, w2, gate, offs, out):
             banks["y", e] = bank
 
         def copy_y(e):
-            if e < 4:
-                flat = raw["w1", 4 + 2 * (e // 2), 0][:].rearrange("p j w -> p (j w)")[:, 0:512].rearrange("p (b n) -> p b n", b=2)
-                y_place[e] = (flat, e // 2 * 2 * C)
+            if e < 6:
+                words = raw["w1", 3 + 2 * (e // 2), 1][:].rearrange("p j w -> p (j w)")[:, 768:1280]
+                y_place[e] = (words.rearrange("p (b n) -> p b n", b=2), e // 2 * 2 * C)
             else:
-                y_place[e] = (y_last[:], 4 * C)
+                y_place[e] = (y_last[:], 6 * C)
             place, base = y_place[e]
             nc.scalar.copy(out=place[:, :, e * C - base : (e + 1) * C - base], in_=banks["y", e][:])
 
@@ -311,98 +307,110 @@ def tile_moe_shr_mlp_silu_kernel(tc, xT, w1, w2, gate, offs, out):
                 start=True,
                 stop=True,
             )
-            tile = ring.tile([P, 512], F32, name="total", tag="total", bufs=4, align_bytes=64)
+            if b == 0:
+                tile = ring.tile([P, T // 2], F32, name="raw_x", tag="raw_x", bufs=4, align_bytes=64)
+            else:
+                tile = ring.tile([P, 512], F32, name="raw_narrow", tag="raw_narrow", bufs=3, align_bytes=64)
             nc.vector.tensor_tensor(tile[:, 0:width], bank[:, 0:width], routed[b][:, cols], ADD)
             nc.sync.dma_start(out=out[rows, cols], in_=tile[:, 0:width])
 
-        for c in range(PASSES):
-            for k in range(3):
-                load_x(c, k)
-        load_w1(SHARED)
-        load_w1(0)
-
-        group_x(0, 0)
-        group_x(0, 1)
-        quantize_x(0, 0)
-        pair_x(0, 0)
-        group_x(0, 2)
-        load_w1(1)
-        load_w2(0)
-        quantize_x(0, 1)
-        pair_x(0, 1)
-        group_x(1, 0)
-        group_x(1, 1)
-        quantize_x(0, 2)
-        pair_x(0, 2)
-        quantize_x(1, 0)
-        pair_x(1, 0)
+        for h in range(2):
+            load_x(0, 0, h)
+        for h in range(2):
+            load_x(0, 1, h)
+        load_w1(SHARED, 0)
+        for h in range(2):
+            pair_x(0, 0, h)
+            load_x(1, 0, h)
+        load_w1(SHARED, 1)
         gather(0, 0, 0)
-        group_x(1, 2)
+        gather(0, 1, 0)
+        for h in range(2):
+            pair_x(0, 1, h)
+            load_x(1, 1, h)
+        load_w1(0, 0)
+        load_w1(0, 1)
+        load_w1(1, 0)
+        load_w1(1, 1)
+        load_w2(0)
         gather(0, 0, 1)
-        quantize_x(1, 1)
-        pair_x(1, 1)
         group_w1(SHARED, 0)
         group_g(0, 0)
-        quantize_x(1, 2)
-        pair_x(1, 2)
-        load_w1(2)
-        load_w2(1)
-        group_w1(SHARED, 1)
-        load_w1(3)
-        load_gates()
+        gather(0, 1, 1)
+        pair_x(1, 0, 0)
+        pair_x(1, 0, 1)
         quantize_g(0, 0)
+        group_g(0, 1)
+        group_x(0, 0)
+        quantize_g(0, 1)
         gather(1, 0, 0)
+        quantize_x(0, 0)
+        group_x(0, 1)
+        group_w1(SHARED, 1)
+        pair_x(1, 1, 0)
+        pair_x(1, 1, 1)
+        gather(1, 1, 0)
+        quantize_x(0, 1)
+        group_x(0, 2)
         gather(1, 0, 1)
+        quantize_x(0, 2)
+        group_g(1, 0)
+        load_w1(2, 0)
+        load_w1(2, 1)
+        load_w2(1)
+        gather(1, 1, 1)
+        quantize_g(1, 0)
+        group_x(1, 0)
+        group_g(1, 1)
+        quantize_x(1, 0)
+        group_x(1, 1)
+        quantize_g(1, 1)
+        quantize_x(1, 1)
+        group_x(1, 2)
+        quantize_x(1, 2)
+        load_gates()
 
-        extra = {
-            0: lambda: (group_g(1, 0), quantize_g(1, 0)),
-            1: lambda: (gather(0, 1, 0), gather(0, 1, 1)),
-            2: lambda: (group_g(0, 1), gather(1, 1, 0), gather(1, 1, 1)),
-            3: lambda: (quantize_g(0, 1), group_g(1, 1)),
-            4: lambda: (quantize_g(1, 1),),
-        }
         for i in range(E + 2):
             prev = SHARED if i == 0 else i - 1
             if i <= E:
                 quantize_w1(prev)
-                if i > 0:
-                    quantize_w2(prev)
+            if i >= 2:
+                quantize_h(i - 2)
+                quantize_w2(i - 2)
+            for q in range(5):
+                if SHARED_STEP[q] == i - 1:
+                    quantize_hs(q)
             if i < E:
                 group_w1(i, 0)
                 group_w1(i, 1)
-            if i in (4, 6, 8):
-                copy_y(i - 4)
-                copy_y(i - 3)
-            if i >= 2:
-                silu_routed(i - 2)
-            if 0 <= i - SH0 - 1 < 5:
-                silu_shared(i - SH0 - 1)
-            if i in PIECES:
-                scatter(0, *PIECES[i])
-            if i >= 2:
-                quantize_h(i - 2)
-            if 0 <= i - SH0 - 1 < 5:
-                quantize_hs(i - SH0 - 1)
-            if i in extra:
-                extra[i]()
             if 1 <= i <= E:
                 multiply1_routed(i - 1)
             if i >= 2:
                 multiply2(i - 2)
-            if 0 <= i - SH0 < 5:
-                multiply1_shared(i - SH0)
+            for q in range(5):
+                if SHARED_STEP[q] == i + 1:
+                    multiply1_shared(q)
+            if 1 <= i <= E:
+                silu_routed(i - 1)
+            for q in range(5):
+                if SHARED_STEP[q] == i:
+                    silu_shared(q)
+            if i in (3, 5, 7):
+                copy_y(i - 3)
+                copy_y(i - 2)
             if i in PIECES:
+                scatter(0, *PIECES[i])
                 scatter(1, *PIECES[i])
-            if i < E:
-                group_w2(i)
-            if i == E - 1:
-                group_w2(SHARED)
+            if 1 <= i <= E:
+                group_w2(i - 1)
             if i == E:
+                group_w2(SHARED)
                 quantize_w2(SHARED)
-            if i + 2 <= E:
+            if i + 3 < E:
+                load_w1(i + 3, 0)
+                load_w1(i + 3, 1)
+            if 1 <= i + 1 and i + 2 <= E:
                 load_w2(i + 2)
-            if 1 <= i and i + 3 < E:
-                load_w1(i + 3)
 
         copy_y(6)
         copy_y(7)

@@ -25,8 +25,8 @@ PASSES = K // PASS
 HALF = 512
 VECTOR_HALF = ((2, 0), (2, 1), (3, 0), (3, 1), (4, 0), (5, 0), (6, 0), (7, 0))
 SCALAR_W2 = (7, 8)
-PIECES = {3: (0, 256), 5: (256, 512), 7: (512, 768)}
-TAIL_PIECES = ((768, 1024),)
+PIECES = {3: (0, 256), 5: (256, 512), 7: (512, 672)}
+TAIL_PIECES = ((672, 1024),)
 SHARED_STEP = (1, 2, 3, 4, 5)
 FINISH = (
     ((0, 512, "bank3"), (512, 512, "bank3"), (1024, 256, "bank_shared")),
@@ -88,6 +88,12 @@ def tile_moe_shr_mlp_silu_kernel(tc, xT, w1, w2, gate, offs, out):
             nc.sync.dma_start(out=tile[:], in_=w2[e].rearrange("(p j) w -> p j w", j=PACK))
             raw["w2", e] = tile
 
+        def interleave_words(dst, src):
+            nc.vector.tensor_copy(
+                out=dst.rearrange("p w t -> p (w t)").bitcast(F32).rearrange("p (c i u) -> p c u i", i=4, u=2),
+                in_=src.rearrange("p u w e -> p u (w e)").bitcast(F32).rearrange("p u (c i) -> p c u i", i=4),
+            )
+
         def interleave(copy, dst, src):
             copy(
                 out=dst.rearrange("p (c i) t -> p c t i", i=4),
@@ -106,10 +112,7 @@ def tile_moe_shr_mlp_silu_kernel(tc, xT, w1, w2, gate, offs, out):
         def group_x(c, k):
             start, width = CHUNKS[k]
             tile = ring.tile([P, 512, PACK], BF16, name="grouped_x", tag="grouped_x", bufs=2, align_bytes=64)
-            nc.vector.tensor_copy(
-                out=tile[:, 0:width, :].rearrange("p w (u e) -> p w u e", e=2),
-                in_=pairs[c][:, :, start : start + width, :].rearrange("p u w e -> p w u e"),
-            )
+            interleave_words(tile[:, 0:width, :], pairs[c][:, :, start : start + width, :])
             grouped["x", c, k] = tile
 
         def quantize_x(c, k):
@@ -134,10 +137,7 @@ def tile_moe_shr_mlp_silu_kernel(tc, xT, w1, w2, gate, offs, out):
 
         def group_g(c, half):
             tile = ring.tile([P, HALF, PACK], BF16, name="grouped_g", tag="grouped_g", bufs=2, align_bytes=64)
-            nc.vector.tensor_copy(
-                out=tile[:].rearrange("p w (u e) -> p w u e", e=2),
-                in_=looked_up[c, half][:].rearrange("p u w e -> p w u e"),
-            )
+            interleave_words(tile[:], looked_up[c, half][:])
             grouped["g", c, half] = tile
 
         def quantize_g(c, half):
@@ -255,8 +255,14 @@ def tile_moe_shr_mlp_silu_kernel(tc, xT, w1, w2, gate, offs, out):
             )
             hidden_codes[e] = (codes, scales)
 
-        y_last = held.tile([P, 2, 2 * C], F32, name="y_last", align_bytes=64)
         y_place = {}
+
+        def next_y(e):
+            if e < 2:
+                return 0, 2, 3
+            if e < 4:
+                return 2, 4, 5
+            return 4, 8, 7
 
         def multiply2(e):
             h_codes, h_scales = hidden_codes[e]
@@ -276,11 +282,9 @@ def tile_moe_shr_mlp_silu_kernel(tc, xT, w1, w2, gate, offs, out):
             banks["y", e] = bank
 
         def copy_y(e):
-            if e < 6:
-                words = raw["w1", 3 + 2 * (e // 2), 1][:].rearrange("p j w -> p (j w)")[:, 768:1280]
-                y_place[e] = (words.rearrange("p (b n) -> p b n", b=2), e // 2 * 2 * C)
-            else:
-                y_place[e] = (y_last[:], 6 * C)
+            first, last, late = next_y(e)
+            words = raw["w1", late, 1][:].rearrange("p j w -> p (j w)")[:, 768 : 768 + 2 * C * (last - first)]
+            y_place[e] = (words.rearrange("p (b n) -> p b n", b=2), first * C)
             place, base = y_place[e]
             nc.scalar.copy(out=place[:, :, e * C - base : (e + 1) * C - base], in_=banks["y", e][:])
 
@@ -390,14 +394,14 @@ def tile_moe_shr_mlp_silu_kernel(tc, xT, w1, w2, gate, offs, out):
             for q in range(5):
                 if SHARED_STEP[q] == i + 1:
                     multiply1_shared(q)
+            if i in (3, 5, 7):
+                copy_y(i - 3)
+                copy_y(i - 2)
             if 1 <= i <= E:
                 silu_routed(i - 1)
             for q in range(5):
                 if SHARED_STEP[q] == i:
                     silu_shared(q)
-            if i in (3, 5, 7):
-                copy_y(i - 3)
-                copy_y(i - 2)
             if i in PIECES:
                 scatter(0, *PIECES[i])
                 scatter(1, *PIECES[i])

from contextlib import ExitStack

import concourse.mybir as mybir

FLOPS = 3019898880

K, T, E, C, H, N = 1024, 1280, 8, 128, 512, 256
S = E * C
SHARED = E

F32 = mybir.dt.float32
BF16 = mybir.dt.bfloat16
U32 = mybir.dt.uint32
U16 = mybir.dt.uint16
U8 = mybir.dt.uint8
FP8X4 = mybir.dt.float8_e4m3fn_x4
SILU = mybir.ActivationFunctionType.Silu
MULT = mybir.AluOpType.mult
ADD = mybir.AluOpType.add

P = 128
PACK = 4
PASS = P * PACK
PASSES = K // PASS
HALF = 512
VECTOR_HALF = ((2, 0), (2, 1), (3, 0), (3, 1), (4, 0), (5, 0), (6, 0), (7, 0))
SCALAR_W2 = (7, 8)
PIECES = {3: (0, 256), 5: (256, 512), 7: (512, 672)}
TAIL_PIECES = ((672, 1024),)
SHARED_STEP = (1, 2, 3, 4, 5)
FINISH = (
    ((0, 512, "bank3"), (512, 512, "bank3"), (1024, 256, "bank_shared")),
    ((0, 512, "bank_shared"), (512, 512, "bank_routed"), (1024, 256, "bank_routed")),
)
CHUNKS = ((0, 512), (512, 512), (1024, 256))
VECTOR_X = ((0, 0, 0), (0, 0, 1))


def tile_moe_shr_mlp_silu_kernel(tc, xT, w1, w2, gate, offs, out):
    nc = tc.nc
    with ExitStack() as ctx:
        lists = ctx.enter_context(tc.tile_pool(name="lists", bufs=1))
        held = ctx.enter_context(tc.tile_pool(name="held", bufs=1))
        ring = ctx.enter_context(tc.tile_pool(name="ring", bufs=2))
        psum = ctx.enter_context(tc.psum_pool(name="psum", bufs=2))

        offsets = lists.tile([P, S // 16], U16, name="offsets")
        nc.sync.dma_start(offsets[:], offs)

        zero = held.tile([P, 1], F32, name="zero")
        zero_out = held.tile([P, 1], F32, name="zero_out")
        nc.vector.memset(zero[:], 0.0)
        nc.scalar.activation(zero_out[:], zero[:], SILU)

        gates = held.tile([P, S], F32, name="gates", align_bytes=64)
        routed = []
        for b in range(2):
            window = held.tile([P, T], F32, name=f"routed{b}", align_bytes=64)
            nc.vector.memset(window[:], 0.0)
            routed.append(window)

        x_codes = held.tile([P, PASSES, T], U32, name="x_codes", align_bytes=64)
        x_scales = held.tile([P, PASSES, T], U8, name="x_scales", align_bytes=64)
        pairs = [held.tile([P, 2, T, 2], BF16, name=f"pairs{c}", align_bytes=64) for c in range(PASSES)]
        g_codes = held.tile([P, PASSES, S], U32, name="g_codes", align_bytes=64)
        g_scales = held.tile([P, PASSES, S], U8, name="g_scales", align_bytes=64)
        hs_codes = held.tile([P, T], U32, name="hs_codes", align_bytes=64)
        hs_scales = held.tile([P, T], U8, name="hs_scales", align_bytes=64)

        raw = {}

        def load_gates():
            nc.sync.dma_start(out=gates[:], in_=gate[0:P, :])

        def load_x(c, u, h):
            tile = ring.tile([P, 2, T // 2], F32, name="raw_x", tag="raw_x", bufs=4, align_bytes=64)
            rows = xT[c * PASS : (c + 1) * PASS, h * (T // 2) : (h + 1) * (T // 2)].rearrange("(p u e) w -> u p e w", u=2, e=2)
            nc.sync.dma_start(out=tile[:], in_=rows[u])
            raw["x", c, u, h] = tile

        def load_w1(e, c):
            tile = ring.tile([P, PACK, H], F32, name="raw_wide", tag="raw_wide", bufs=7, align_bytes=64)
            nc.sync.dma_start(out=tile[:], in_=w1[e, c * PASS : (c + 1) * PASS, :].rearrange("(p j) w -> p j w", j=PACK))
            raw["w1", e, c] = tile

        def load_w2(e):
            tile = ring.tile([P, PACK, N], F32, name="raw_narrow", tag="raw_narrow", bufs=3, align_bytes=64)
            nc.sync.dma_start(out=tile[:], in_=w2[e].rearrange("(p j) w -> p j w", j=PACK))
            raw["w2", e] = tile

        def interleave_words(dst, src):
            nc.vector.tensor_copy(
                out=dst.rearrange("p w t -> p (w t)").bitcast(F32).rearrange("p (c i u) -> p c u i", i=4, u=2),
                in_=src.rearrange("p u w e -> p u (w e)").bitcast(F32).rearrange("p u (c i) -> p c u i", i=4),
            )

        def interleave(copy, dst, src):
            copy(
                out=dst.rearrange("p (c i) t -> p c t i", i=4),
                in_=src.rearrange("p t (c i) -> p c t i", i=4),
            )

        grouped = {}

        def pair_x(c, u, h):
            copy = nc.vector.tensor_copy if (c, u, h) in VECTOR_X else nc.scalar.copy
            copy(
                out=pairs[c][:, u, h * (T // 2) : (h + 1) * (T // 2), :].rearrange("p (c i) e -> p c e i", i=4),
                in_=raw["x", c, u, h][:].rearrange("p e (c i) -> p c e i", i=4),
            )

        def group_x(c, k):
            start, width = CHUNKS[k]
            tile = ring.tile([P, 512, PACK], BF16, name="grouped_x", tag="grouped_x", bufs=2, align_bytes=64)
            interleave_words(tile[:, 0:width, :], pairs[c][:, :, start : start + width, :])
            grouped["x", c, k] = tile

        def quantize_x(c, k):
            start, width = CHUNKS[k]
            cols = slice(start, start + width)
            nc.vector.quantize_mx(
                out=x_codes[:, c, cols].bitcast(FP8X4),
                scales=x_scales[:, c, cols],
                in_=grouped["x", c, k][:, 0:width, :].rearrange("p w t -> p (w t)"),
            )

        looked_up = {}

        def gather(c, half, u):
            if u == 0:
                looked_up[c, half] = ring.tile([P, 2, HALF, 2], BF16, name="gathered", tag="gathered", bufs=2, align_bytes=64)
            window = pairs[c][:, u, :, :].rearrange("p t e -> p (t e)").bitcast(U32)
            nc.vector.tensor_copy(
                out=looked_up[c, half][:, u, :, :].rearrange("p t e -> p (t e)").bitcast(U32),
                in_=window.indirect(offsets[:, half * (HALF // 16) : (half + 1) * (HALF // 16)]),
            )

        def group_g(c, half):
            tile = ring.tile([P, HALF, PACK], BF16, name="grouped_g", tag="grouped_g", bufs=2, align_bytes=64)
            interleave_words(tile[:], looked_up[c, half][:])
            grouped["g", c, half] = tile

        def quantize_g(c, half):
            cols = slice(half * HALF, (half + 1) * HALF)
            nc.vector.quantize_mx(
                out=g_codes[:, c, cols].bitcast(FP8X4),
                scales=g_scales[:, c, cols],
                in_=grouped["g", c, half][:].rearrange("p w t -> p (w t)"),
            )

        def group_w1(e, c):
            tile = ring.tile([P, PACK * H], BF16, name="grouped_w1", tag="grouped_w1", bufs=6, align_bytes=64)
            dst = tile[:].rearrange("p (t m j) -> p m j t", t=PACK, j=PACK)
            src = raw["w1", e, c][:].rearrange("p j (m t) -> p m j t", t=PACK)
            if (e, c) in VECTOR_HALF:
                nc.vector.tensor_copy(out=dst[:, :, :, 0:2], in_=src[:, :, :, 0:2])
                nc.scalar.copy(out=dst[:, :, :, 2:4], in_=src[:, :, :, 2:4])
            else:
                nc.scalar.copy(out=dst, in_=src)
            grouped["w1", e, c] = tile

        def group_w2(e):
            copy = nc.scalar.copy if e in SCALAR_W2 else nc.vector.tensor_copy
            tile = ring.tile([P, N, PACK], BF16, name="grouped_w2", tag="grouped_w2", bufs=3, align_bytes=64)
            interleave(copy, tile[:], raw["w2", e][:])
            grouped["w2", e] = tile

        weights = {}

        def quantize_w1(e):
            if e == SHARED:
                codes = held.tile([P, PASSES, H], U32, name="shared_codes", align_bytes=64)
                scales = held.tile([P, PASSES, H], U8, name="shared_scales", align_bytes=64)
            else:
                codes = ring.tile([P, PASSES, H], U32, name="w1_codes", tag="w1_codes", bufs=2, align_bytes=64)
                scales = ring.tile([P, PASSES, H], U8, name="w1_scales", tag="w1_scales", bufs=2, align_bytes=64)
            for c in range(PASSES):
                nc.vector.quantize_mx(out=codes[:, c, :].bitcast(FP8X4), scales=scales[:, c, :], in_=grouped["w1", e, c][:])
            weights["w1", e] = (codes, scales)

        def quantize_w2(e):
            codes = ring.tile([P, N], U32, name="w2_codes", tag="w2_codes", bufs=4, align_bytes=64)
            scales = ring.tile([P, N], U8, name="w2_scales", tag="w2_scales", bufs=4, align_bytes=64)
            nc.vector.quantize_mx(
                out=codes[:].bitcast(FP8X4), scales=scales[:], in_=grouped["w2", e][:].rearrange("p w t -> p (w t)")
            )
            weights["w2", e] = (codes, scales)

        banks = {}
        hidden = {}

        def multiply1(key, e, codes, scales, start, tag):
            w_codes, w_scales = weights["w1", e]
            cols = slice(start, start + C)
            bank = psum.tile([P, PACK, C], F32, name="bank1", tag=tag, bufs=2)
            for t in range(PACK):
                for c in range(PASSES):
                    rows = slice(t * P, (t + 1) * P)
                    nc.tensor.matmul_mx(
                        out=bank[:, t, :],
                        lhsT=w_codes[:, c, rows].bitcast(FP8X4),
                        lhsT_scale=w_scales[:, c, rows],
                        rhs=codes[:, c, cols].bitcast(FP8X4),
                        rhs_scale=scales[:, c, cols],
                        start=(c == 0),
                        stop=(c == PASSES - 1),
                    )
            banks[key] = bank

        def multiply1_routed(e):
            multiply1(e, e, g_codes, g_scales, e * C, "bank_routed")

        def multiply1_shared(q):
            for n in (2 * q, 2 * q + 1):
                multiply1(("s", n), SHARED, x_codes, x_scales, n * C, "bank_shared")

        def freed(e, c, first, last):
            return raw["w1", e, c][:].rearrange("p j w -> p (j w)")[:, first:last].bitcast(BF16).rearrange("p (n t) -> p n t", t=PACK)

        def silu_routed(e):
            if e + 1 < E:
                hidden[e] = freed(e + 1, 1, 0, 256)
            else:
                tile = ring.tile([P, C, PACK], BF16, name="hidden_routed", tag="hidden_routed", bufs=2, align_bytes=64)
                hidden[e] = tile[:]
            nc.scalar.activation(hidden[e], banks[e][:].rearrange("p t n -> p n t"), SILU)

        def silu_shared(q):
            if SHARED_STEP[q] < E:
                tile = freed(SHARED_STEP[q], 1, 256, 768)
            else:
                own = ring.tile([P, 2 * C, PACK], BF16, name="hidden_shared", tag="hidden_shared", bufs=2, align_bytes=64)
                tile = own[:]
            for part in range(2):
                nc.scalar.activation(
                    tile[:, part * C : (part + 1) * C, :], banks["s", 2 * q + part][:].rearrange("p t n -> p n t"), SILU
                )
            hidden["s", q] = tile

        def quantize_hs(q):
            cols = slice(q * 2 * C, (q + 1) * 2 * C)
            nc.vector.quantize_mx(
                out=hs_codes[:, cols].bitcast(FP8X4),
                scales=hs_scales[:, cols],
                in_=hidden["s", q].rearrange("p w t -> p (w t)"),
            )

        hidden_codes = {}

        def quantize_h(e):
            codes = ring.tile([P, C], U32, name="h_codes", tag="h_codes", bufs=3, align_bytes=64)
            scales = ring.tile([P, C], U8, name="h_scales", tag="h_scales", bufs=3, align_bytes=64)
            nc.vector.quantize_mx(
                out=codes[:].bitcast(FP8X4), scales=scales[:], in_=hidden[e].rearrange("p w t -> p (w t)")
            )
            hidden_codes[e] = (codes, scales)

        y_place = {}

        def next_y(e):
            if e < 2:
                return 0, 2, 3
            if e < 4:
                return 2, 4, 5
            return 4, 8, 7

        def multiply2(e):
            h_codes, h_scales = hidden_codes[e]
            w_codes, w_scales = weights["w2", e]
            bank = psum.tile([P, 2, C], F32, name="bank2", tag="bank2", bufs=2)
            for b in range(2):
                rows = slice(b * P, (b + 1) * P)
                nc.tensor.matmul_mx(
                    out=bank[:, b, :],
                    lhsT=w_codes[:, rows].bitcast(FP8X4),
                    lhsT_scale=w_scales[:, rows],
                    rhs=h_codes[:].bitcast(FP8X4),
                    rhs_scale=h_scales[:],
                    start=True,
                    stop=True,
                )
            banks["y", e] = bank

        def copy_y(e):
            first, last, late = next_y(e)
            words = raw["w1", late, 1][:].rearrange("p j w -> p (j w)")[:, 768 : 768 + 2 * C * (last - first)]
            y_place[e] = (words.rearrange("p (b n) -> p b n", b=2), first * C)
            place, base = y_place[e]
            nc.scalar.copy(out=place[:, :, e * C - base : (e + 1) * C - base], in_=banks["y", e][:])

        def scatter(b, first, last):
            place, base = y_place[first // C]
            nc.vector.tensor_tensor(
                routed[b][:].indirect(offsets[:, first // 16 : last // 16]),
                place[:, b, first - base : last - base],
                gates[:, first:last],
                MULT,
            )

        def finish(b, start, width, tag):
            w_codes, w_scales = weights["w2", SHARED]
            rows = slice(b * P, (b + 1) * P)
            cols = slice(start, start + width)
            bank = psum.tile([P, 512], F32, name="bank3", tag=tag, bufs=2)
            nc.tensor.matmul_mx(
                out=bank[:, 0:width],
                lhsT=w_codes[:, rows].bitcast(FP8X4),
                lhsT_scale=w_scales[:, rows],
                rhs=hs_codes[:, cols].bitcast(FP8X4),
                rhs_scale=hs_scales[:, cols],
                start=True,
                stop=True,
            )
            if b == 0:
                tile = ring.tile([P, T // 2], F32, name="raw_x", tag="raw_x", bufs=4, align_bytes=64)
            else:
                tile = ring.tile([P, 512], F32, name="raw_narrow", tag="raw_narrow", bufs=3, align_bytes=64)
            nc.vector.tensor_tensor(tile[:, 0:width], bank[:, 0:width], routed[b][:, cols], ADD)
            nc.sync.dma_start(out=out[rows, cols], in_=tile[:, 0:width])

        for h in range(2):
            load_x(0, 0, h)
        for h in range(2):
            load_x(0, 1, h)
        load_w1(SHARED, 0)
        for h in range(2):
            pair_x(0, 0, h)
            load_x(1, 0, h)
        load_w1(SHARED, 1)
        gather(0, 0, 0)
        gather(0, 1, 0)
        for h in range(2):
            pair_x(0, 1, h)
            load_x(1, 1, h)
        load_w1(0, 0)
        load_w1(0, 1)
        load_w1(1, 0)
        load_w1(1, 1)
        load_w2(0)
        gather(0, 0, 1)
        group_w1(SHARED, 0)
        group_g(0, 0)
        gather(0, 1, 1)
        pair_x(1, 0, 0)
        pair_x(1, 0, 1)
        quantize_g(0, 0)
        group_g(0, 1)
        group_x(0, 0)
        quantize_g(0, 1)
        gather(1, 0, 0)
        quantize_x(0, 0)
        group_x(0, 1)
        group_w1(SHARED, 1)
        pair_x(1, 1, 0)
        pair_x(1, 1, 1)
        gather(1, 1, 0)
        quantize_x(0, 1)
        group_x(0, 2)
        gather(1, 0, 1)
        quantize_x(0, 2)
        group_g(1, 0)
        load_w1(2, 0)
        load_w1(2, 1)
        load_w2(1)
        gather(1, 1, 1)
        quantize_g(1, 0)
        group_x(1, 0)
        group_g(1, 1)
        quantize_x(1, 0)
        group_x(1, 1)
        quantize_g(1, 1)
        quantize_x(1, 1)
        group_x(1, 2)
        quantize_x(1, 2)
        load_gates()

        for i in range(E + 2):
            prev = SHARED if i == 0 else i - 1
            if i <= E:
                quantize_w1(prev)
            if i >= 2:
                quantize_h(i - 2)
                quantize_w2(i - 2)
            for q in range(5):
                if SHARED_STEP[q] == i - 1:
                    quantize_hs(q)
            if i < E:
                group_w1(i, 0)
                group_w1(i, 1)
            if 1 <= i <= E:
                multiply1_routed(i - 1)
            if i >= 2:
                multiply2(i - 2)
            for q in range(5):
                if SHARED_STEP[q] == i + 1:
                    multiply1_shared(q)
            if i in (3, 5, 7):
                copy_y(i - 3)
                copy_y(i - 2)
            if 1 <= i <= E:
                silu_routed(i - 1)
            for q in range(5):
                if SHARED_STEP[q] == i:
                    silu_shared(q)
            if i in PIECES:
                scatter(0, *PIECES[i])
                scatter(1, *PIECES[i])
            if 1 <= i <= E:
                group_w2(i - 1)
            if i == E:
                group_w2(SHARED)
                quantize_w2(SHARED)
            if i + 3 < E:
                load_w1(i + 3, 0)
                load_w1(i + 3, 1)
            if 1 <= i + 1 and i + 2 <= E:
                load_w2(i + 2)

        copy_y(6)
        copy_y(7)
        for b in range(2):
            for piece in TAIL_PIECES:
                scatter(b, *piece)
            for start, width, tag in FINISH[b]:
                finish(b, start, width, tag)
